import numpy as np, ml_dtypes
CORES = [0,8,16,24,32,40,48,56,64,72,80,88,96,104,112,120]
N = 16
GROUPS = [[0,8],[1,9],[2,10],[3,11],[4,12],[5,13],[6,14],[7,15]]
def setup_inputs(rng):
    return {"x": rng.standard_normal((N, 128, 2048), dtype=np.float32).astype(ml_dtypes.bfloat16)}
def reference(x):
    y = np.empty((N, 128, 2048), x.dtype)
    for g in GROUPS:
        s = x[g].max(axis=0)
        for r in g:
            y[r] = s
    return {"y": y}

@@ -1,0 +1,86 @@
+import concourse.bass as bass
+
+RF = 64
+RD = 128 - RF
+F_HELP = [4, 5, 6, 7]
+D_HELP = [1, 2]
+NF, ND = len(F_HELP), len(D_HELP)
+WF = RF * 2048 // (NF * 128)
+WD = RD * 2048 // (ND * 128)
+
+SCRATCH = {
+    "xsF": ("dram", [NF, 128, WF], "bfloat16"),
+    "xsD": ("dram", [ND, 128, WD], "bfloat16"),
+    "resF": ("dram", [NF, 128, WF], "bfloat16"),
+    "resD": ("dram", [ND, 128, WD], "bfloat16"),
+    "ownF": ("dram", [128, WF], "bfloat16"),
+    "peerF": ("dram", [128, WF], "bfloat16"),
+    "ownD": ("dram", [128, WD], "bfloat16"),
+    "peerD": ("dram", [128, WD], "bfloat16"),
+}
+SEMAPHORES = ["ldF", "ldD", "st", "sent", "own", "peer", "gotF", "gotD"]
+
+
+def rank_program(g, core, T, topo):
+    chip, k = topo.chip(core), core % 8
+    home_of = {topo.chip(c): c for c in T.cores}
+    if chip not in home_of:
+        return
+    home = home_of[chip]
+    rank = T.rank_of(home)
+    grp = [m for m in T.tables["GROUPS"] if rank in m][0]
+    other = T.cores[[r for r in grp if r != rank][0]]
+    S = T.sem
+
+    def dst(c):
+        rid, pid, se = topo.addr(c)
+        return bass.DstId(rid=rid, pnc=pid)
+
+    def here(j):
+        return chip * 8 + j
+
+    def there(j):
+        return topo.chip(other) * 8 + j
+
+    if core == home:
+        g.dma_start(T.xsF[:], T.x[0:RF, :]).then_inc(S.ldF, 16)
+        g.dma_start(T.xsD[:], T.x[RF:128, :]).then_inc(S.ldD, 16)
+        g.wait_ge(S.ldF, 16)
+        eF = 16 // NF
+        g.remote_dma_fused(
+            [bass.RemoteDMATransfer(dst_ids=[dst(here(h))], dma_engine_mask=((1 << eF) - 1) << (i * eF),
+                                    remote_sem=S.own, src=T.xsF[i], dst=T.ownF[:])
+             for i, h in enumerate(F_HELP)], local_sem=S.sent)
+        g.wait_ge(S.ldD, 16)
+        eD = 8 // ND
+        g.remote_dma_fused(
+            [bass.RemoteDMATransfer(dst_ids=[dst(there(h))], dma_engine_mask=((1 << eD) - 1) << (i * eD),
+                                    remote_sem=S.peer, src=T.xsD[i], dst=T.peerD[:])
+             for i, h in enumerate(D_HELP)] +
+            [bass.RemoteDMATransfer(dst_ids=[dst(here(h))], dma_engine_mask=((1 << eD) - 1) << (8 + i * eD),
+                                    remote_sem=S.own, src=T.xsD[i], dst=T.ownD[:])
+             for i, h in enumerate(D_HELP)], local_sem=S.sent)
+        g.wait_ge(S.gotD, 16 * ND)
+        g.dma_start(T.y[RF:128, :], T.resD[:]).then_inc(S.st, 16)
+        g.wait_ge(S.gotF, 16 * NF)
+        g.dma_start(T.y[0:RF, :], T.resF[:]).then_inc(S.st, 16)
+        g.wait_ge(S.sent, 32)
+        g.wait_ge(S.st, 32)
+    elif k in F_HELP:
+        i = F_HELP.index(k)
+        rid, pid, se = topo.addr(there(k))
+        g.wait_ge(S.own, 16 // NF)
+        g.remote_dma(T.peerF[:], T.ownF[:], S.peer, S.sent, pid, rid, 0x00FF)
+        g.wait_ge(S.peer, 8)
+        g.remote_dma_fused(
+            [bass.RemoteDMATransfer(dst_ids=[dst(home)], dma_engine_mask=0xFFFF, remote_sem=S.gotF,
+                                    srcs=[T.ownF[:], T.peerF[:]], dsts=[T.resF[i]], alu_op=2)], local_sem=S.sent)
+        g.wait_ge(S.sent, 24)
+    elif k in D_HELP:
+        i = D_HELP.index(k)
+        g.wait_ge(S.own, 8 // ND)
+        g.wait_ge(S.peer, 8 // ND)
+        g.remote_dma_fused(
+            [bass.RemoteDMATransfer(dst_ids=[dst(home)], dma_engine_mask=0xFFFF, remote_sem=S.gotD,
+                                    srcs=[T.ownD[:], T.peerD[:]], dsts=[T.resD[i]], alu_op=2)], local_sem=S.sent)
+        g.wait_ge(S.sent, 16)

@@ -1,18 +1,18 @@
 import concourse.bass as bass
 
-RF = 64
+RF = 56
 RD = 128 - RF
 F_HELP = [4, 5, 6, 7]
 D_HELP = [1, 2]
 NF, ND = len(F_HELP), len(D_HELP)
 WF = RF * 2048 // (NF * 128)
-WD = RD * 2048 // (ND * 128)
+WD = RD * 2048 // (2 * ND * 128)
 
 SCRATCH = {
     "xsF": ("dram", [NF, 128, WF], "bfloat16"),
-    "xsD": ("dram", [ND, 128, WD], "bfloat16"),
+    "xsD": ("dram", [2 * ND, 128, WD], "bfloat16"),
     "resF": ("dram", [NF, 128, WF], "bfloat16"),
-    "resD": ("dram", [ND, 128, WD], "bfloat16"),
+    "resD": ("dram", [2 * ND, 128, WD], "bfloat16"),
     "ownF": ("dram", [128, WF], "bfloat16"),
     "peerF": ("dram", [128, WF], "bfloat16"),
     "ownD": ("dram", [128, WD], "bfloat16"),
@@ -30,6 +30,7 @@ def rank_program(g, core, T, topo):
     rank = T.rank_of(home)
     grp = [m for m in T.tables["GROUPS"] if rank in m][0]
     other = T.cores[[r for r in grp if r != rank][0]]
+    side = 0 if home < other else 1
     S = T.sem
 
     def dst(c):
@@ -55,12 +56,12 @@ def rank_program(g, core, T, topo):
         eD = 8 // ND
         g.remote_dma_fused(
             [bass.RemoteDMATransfer(dst_ids=[dst(there(h))], dma_engine_mask=((1 << eD) - 1) << (i * eD),
-                                    remote_sem=S.peer, src=T.xsD[i], dst=T.peerD[:])
+                                    remote_sem=S.peer, src=T.xsD[ND * (1 - side) + i], dst=T.peerD[:])
              for i, h in enumerate(D_HELP)] +
             [bass.RemoteDMATransfer(dst_ids=[dst(here(h))], dma_engine_mask=((1 << eD) - 1) << (8 + i * eD),
-                                    remote_sem=S.own, src=T.xsD[i], dst=T.ownD[:])
+                                    remote_sem=S.own, src=T.xsD[ND * side + i], dst=T.ownD[:])
              for i, h in enumerate(D_HELP)], local_sem=S.sent)
-        g.wait_ge(S.gotD, 16 * ND)
+        g.wait_ge(S.gotD, 8 * 2 * ND)
         g.dma_start(T.y[RF:128, :], T.resD[:]).then_inc(S.st, 16)
         g.wait_ge(S.gotF, 16 * NF)
         g.dma_start(T.y[0:RF, :], T.resF[:]).then_inc(S.st, 16)
@@ -77,10 +78,12 @@ def rank_program(g, core, T, topo):
                                     srcs=[T.ownF[:], T.peerF[:]], dsts=[T.resF[i]], alu_op=2)], local_sem=S.sent)
         g.wait_ge(S.sent, 24)
     elif k in D_HELP:
-        i = D_HELP.index(k)
+        p = ND * side + D_HELP.index(k)
         g.wait_ge(S.own, 8 // ND)
         g.wait_ge(S.peer, 8 // ND)
         g.remote_dma_fused(
-            [bass.RemoteDMATransfer(dst_ids=[dst(home)], dma_engine_mask=0xFFFF, remote_sem=S.gotD,
-                                    srcs=[T.ownD[:], T.peerD[:]], dsts=[T.resD[i]], alu_op=2)], local_sem=S.sent)
+            [bass.RemoteDMATransfer(dst_ids=[dst(other)], dma_engine_mask=0x00FF, remote_sem=S.gotD,
+                                    srcs=[T.ownD[:], T.peerD[:]], dsts=[T.resD[p]], alu_op=2),
+             bass.RemoteDMATransfer(dst_ids=[dst(home)], dma_engine_mask=0xFF00, remote_sem=S.gotD,
+                                    srcs=[T.ownD[:], T.peerD[:]], dsts=[T.resD[p]], alu_op=2)], local_sem=S.sent)
         g.wait_ge(S.sent, 16)

import concourse.bass as bass

RF = 56
RD = 128 - RF
F_HELP = [4, 5, 6, 7]
D_HELP = [1, 2]
NF, ND = len(F_HELP), len(D_HELP)
WF = RF * 2048 // (NF * 128)
WD = RD * 2048 // (2 * ND * 128)

SCRATCH = {
    "xsF": ("dram", [NF, 128, WF], "bfloat16"),
    "xsD": ("dram", [2 * ND, 128, WD], "bfloat16"),
    "resF": ("dram", [NF, 128, WF], "bfloat16"),
    "resD": ("dram", [2 * ND, 128, WD], "bfloat16"),
    "ownF": ("dram", [128, WF], "bfloat16"),
    "peerF": ("dram", [128, WF], "bfloat16"),
    "ownD": ("dram", [128, WD], "bfloat16"),
    "peerD": ("dram", [128, WD], "bfloat16"),
}
SEMAPHORES = ["ldF", "ldD", "st", "sent", "own", "peer", "gotF", "gotD"]


def rank_program(g, core, T, topo):
    chip, k = topo.chip(core), core % 8
    home_of = {topo.chip(c): c for c in T.cores}
    if chip not in home_of:
        return
    home = home_of[chip]
    rank = T.rank_of(home)
    grp = [m for m in T.tables["GROUPS"] if rank in m][0]
    other = T.cores[[r for r in grp if r != rank][0]]
    side = 0 if home < other else 1
    S = T.sem

    def dst(c):
        rid, pid, se = topo.addr(c)
        return bass.DstId(rid=rid, pnc=pid)

    def here(j):
        return chip * 8 + j

    def there(j):
        return topo.chip(other) * 8 + j

    if core == home:
        g.dma_start(T.xsF[:], T.x[0:RF, :]).then_inc(S.ldF, 16)
        g.dma_start(T.xsD[:], T.x[RF:128, :]).then_inc(S.ldD, 16)
        g.wait_ge(S.ldF, 16)
        eF = 16 // NF
        g.remote_dma_fused(
            [bass.RemoteDMATransfer(dst_ids=[dst(here(h))], dma_engine_mask=((1 << eF) - 1) << (i * eF),
                                    remote_sem=S.own, src=T.xsF[i], dst=T.ownF[:])
             for i, h in enumerate(F_HELP)], local_sem=S.sent)
        g.wait_ge(S.ldD, 16)
        eD = 8 // ND
        g.remote_dma_fused(
            [bass.RemoteDMATransfer(dst_ids=[dst(there(h))], dma_engine_mask=((1 << eD) - 1) << (i * eD),
                                    remote_sem=S.peer, src=T.xsD[ND * (1 - side) + i], dst=T.peerD[:])
             for i, h in enumerate(D_HELP)] +
            [bass.RemoteDMATransfer(dst_ids=[dst(here(h))], dma_engine_mask=((1 << eD) - 1) << (8 + i * eD),
                                    remote_sem=S.own, src=T.xsD[ND * side + i], dst=T.ownD[:])
             for i, h in enumerate(D_HELP)], local_sem=S.sent)
        g.wait_ge(S.gotD, 8 * 2 * ND)
        g.dma_start(T.y[RF:128, :], T.resD[:]).then_inc(S.st, 16)
        g.wait_ge(S.gotF, 16 * NF)
        g.dma_start(T.y[0:RF, :], T.resF[:]).then_inc(S.st, 16)
        g.wait_ge(S.sent, 32)
        g.wait_ge(S.st, 32)
    elif k in F_HELP:
        i = F_HELP.index(k)
        rid, pid, se = topo.addr(there(k))
        g.wait_ge(S.own, 16 // NF)
        g.remote_dma(T.peerF[:], T.ownF[:], S.peer, S.sent, pid, rid, 0x00FF)
        g.wait_ge(S.peer, 8)
        g.remote_dma_fused(
            [bass.RemoteDMATransfer(dst_ids=[dst(home)], dma_engine_mask=0xFFFF, remote_sem=S.gotF,
                                    srcs=[T.ownF[:], T.peerF[:]], dsts=[T.resF[i]], alu_op=2)], local_sem=S.sent)
        g.wait_ge(S.sent, 24)
    elif k in D_HELP:
        p = ND * side + D_HELP.index(k)
        g.wait_ge(S.own, 8 // ND)
        g.wait_ge(S.peer, 8 // ND)
        g.remote_dma_fused(
            [bass.RemoteDMATransfer(dst_ids=[dst(other)], dma_engine_mask=0x00FF, remote_sem=S.gotD,
                                    srcs=[T.ownD[:], T.peerD[:]], dsts=[T.resD[p]], alu_op=2),
             bass.RemoteDMATransfer(dst_ids=[dst(home)], dma_engine_mask=0xFF00, remote_sem=S.gotD,
                                    srcs=[T.ownD[:], T.peerD[:]], dsts=[T.resD[p]], alu_op=2)], local_sem=S.sent)
        g.wait_ge(S.sent, 16)
